import numpy as np
import ml_dtypes


def mxq(x, axis, fmt="e4m3"):
    dtype, down = {"e4m3": (ml_dtypes.float8_e4m3fn, 7), "e5m2": (ml_dtypes.float8_e5m2, 14)}[fmt]
    v = np.moveaxis(np.asarray(x, np.float32).astype(ml_dtypes.bfloat16).astype(np.float64), axis, -1)
    blocks = v.reshape(v.shape[:-1] + (-1, 32))
    amax = np.abs(blocks).max(-1, keepdims=True)
    byte = np.maximum(np.where(amax > 0, np.frexp(amax)[1] - 1 + 127, 0) - down, 1)
    scale = np.exp2(byte - 127.0)
    codes = (blocks / scale).astype(np.float32).astype(dtype).astype(np.float64)
    return np.moveaxis((codes * scale).reshape(v.shape), -1, axis)


WIDE = False


def mx_kscale(k):
    if not WIDE:
        return np.ones(k)
    levels = np.array([10, -10, 5, -5, 0])
    if k % 512:
        return np.exp2(np.random.permutation(np.resize(levels, k // 32))).repeat(32)
    a = np.empty((k // 512, 16))
    for p in range(k // 512):
        a[p, :8] = np.random.permutation(np.resize(levels, 8))
        for g in range(8):
            far = levels[np.abs(levels - a[p, g]) >= 10]
            a[p, g + 8] = far[np.random.randint(len(far))]
    return np.exp2(a.ravel()).repeat(32)


BF16 = ml_dtypes.bfloat16


def bf(x):
    return np.asarray(x, np.float32).astype(BF16)


def f64(x):
    return np.asarray(x).astype(np.float64)


E2M1 = np.array([0.0, 0.5, 1.0, 1.5, 2.0, 3.0, 4.0, 6.0, -0.0, -0.5, -1.0, -1.5, -2.0, -3.0, -4.0, -6.0])


def pack_weight(w, fmt):
    k, n = w.shape
    w = f64(bf(w)).reshape(k // 32, 32, n)
    amax = np.abs(w).max(1)
    if fmt == "e4m3":
        byte = np.frexp(amax)[1] - 1 + 127 - 7
    else:
        mant, ex = np.frexp(amax / 6.0)
        byte = np.where(mant > 0.5, ex, ex - 1) + 127
    byte = np.clip(np.where(amax > 0, byte, 1), 1, 254)
    scaled = (w * np.exp2(127.0 - byte)[:, None, :]).reshape(k, n).astype(np.float32)
    by_word = np.ascontiguousarray(scaled.reshape(k // 512, 128, 4, n).transpose(0, 1, 3, 2))
    if fmt == "e4m3":
        words = by_word.astype(ml_dtypes.float8_e4m3fn).view(np.uint8)
    else:
        c = by_word.astype(ml_dtypes.float4_e2m1fn).view(np.uint8) & 0xF
        words = c[..., 0::2] | (c[..., 1::2] << 4)
    return np.ascontiguousarray(words), np.ascontiguousarray(byte.astype(np.uint8).reshape(k // 512, 16, n))


def unpack_weight(words, scales, fmt):
    g, p, n, _ = words.shape
    if fmt == "e4m3":
        vals = np.ascontiguousarray(words).view(ml_dtypes.float8_e4m3fn).astype(np.float64)
    else:
        nib = np.empty((g, p, n, 4), np.uint8)
        nib[..., 0::2] = words & 0xF
        nib[..., 1::2] = words >> 4
        vals = E2M1[nib]
    vals = vals * np.repeat(np.exp2(scales.astype(np.float64) - 127.0), 8, axis=1)[..., None]
    return vals.transpose(0, 1, 3, 2).reshape(g * 512, n)


B, D, H = 1024, 512, 1024
H3 = 3 * H


def sigmoid(v):
    return 1.0 / (1.0 + np.exp(-v))


def _hidden_decay(delta, wg_words, wg_scales, bg):
    p = mxq(f64(delta), 1, "e4m3") @ unpack_weight(wg_words, wg_scales, "e4m3")
    return np.exp(-np.maximum(0.0, p + f64(bg)))


def _three_blocks(a, n):
    return a[:, :n], a[:, n:2 * n], a[:, 2 * n:]


def draw0():
    s, t = mx_kscale(D), mx_kscale(H)
    xp = bf(np.random.standard_normal((B, H3)) * 0.7)
    delta = bf(np.random.standard_normal((B, D)) * s)
    h = bf(np.random.standard_normal((B, H)))
    wg_words, wg_scales = pack_weight(np.random.standard_normal((D, H)) / np.sqrt(D) / s[:, None], "e4m3")
    bg = bf(np.random.standard_normal(H) * 0.3)
    g = bf((1.0 + 0.2 * np.random.standard_normal(H)) * t)
    u_words, u_scales = pack_weight(np.random.standard_normal((H, H3)) / np.sqrt(H) / t[:, None], "e4m3")
    return {
        "xp": xp,
        "delta": delta,
        "h": h,
        "wg_words": wg_words,
        "wg_scales": wg_scales,
        "bg": bg,
        "g": g,
        "u_words": u_words,
        "u_scales": u_scales,
    }


def core(xp, delta, h, wg_words, wg_scales, bg, g, u_words, u_scales):
    n = h.shape[-1]
    gamma = _hidden_decay(delta, wg_words, wg_scales, bg)
    hd = gamma * f64(h)
    q = mxq(hd * f64(g)[None, :], 1, "e4m3") @ unpack_weight(u_words, u_scales, "e4m3")
    xz, xr, xc = _three_blocks(f64(xp), n)
    qz, qr, qc = _three_blocks(q, n)
    z = sigmoid(xz + qz)
    r = sigmoid(xr + qr)
    cand = np.tanh(xc + r * qc)
    return (1.0 - z) * hd + z * cand


def e4m3fn_bytes(y):
    return np.clip(np.asarray(y, np.float64), -448.0, 448.0).astype(np.float32).astype(ml_dtypes.float8_e4m3fn).view(np.uint8)


def e4m3fn_values(b):
    return np.asarray(b, np.uint8).view(ml_dtypes.float8_e4m3fn).astype(np.float64)


def setup_inputs():
    d = draw0()
    x0 = np.asarray(d['delta']).astype(np.float64)
    s = (np.max(np.abs(x0), axis=(0,), keepdims=True) / 448.0).astype(np.float32)
    out = {}
    for k, v in d.items():
        if k == 'delta':
            out['delta_bytes'] = e4m3fn_bytes(x0 / s.astype(np.float64))
            out['delta_scale'] = s
        else:
            out[k] = v
    return out


def reference(xp, delta_bytes, delta_scale, h, wg_words, wg_scales, bg, g, u_words, u_scales):
    return core(xp, e4m3fn_values(delta_bytes) * delta_scale.astype(np.float64), h, wg_words, wg_scales, bg, g, u_words, u_scales)

@@ -1,0 +1,344 @@
+from contextlib import ExitStack
+
+import concourse.mybir as mybir
+from concourse.masks import make_identity
+
+B, D, H = 1024, 512, 1024
+FLOPS = 2 * B * D * H + 2 * B * H * 3 * H
+
+F32 = mybir.dt.float32
+BF16 = mybir.dt.bfloat16
+I32 = mybir.dt.int32
+U32 = mybir.dt.uint32
+U8 = mybir.dt.uint8
+FP8 = mybir.dt.float8_e4m3fn
+FP8X4 = mybir.dt.float8_e4m3fn_x4
+ACT = mybir.ActivationFunctionType
+ALU = mybir.AluOpType
+
+P = 128
+PACK = 4
+KP = P * PACK
+TILES = B // P
+CHUNK = 512
+CHUNKS = B // CHUNK
+TPC = CHUNK // P
+GROUPS = H // KP
+PAIR = 2 * P
+UNITS = TILES * GROUPS
+Z, R, C = 0, 1, 2
+
+
+def tile_grudhiddendecayresetafterstep_w8_kernel(
+    tc, xp, delta_bytes, delta_scale, h, wg_words, wg_scales, bg, g, u_words, u_scales, out
+):
+    nc = tc.nc
+    with ExitStack() as ctx:
+        keep = ctx.enter_context(tc.tile_pool(name="keep", bufs=1))
+        work = ctx.enter_context(tc.tile_pool(name="work", bufs=4))
+        psum = ctx.enter_context(tc.psum_pool(name="psum", bufs=2))
+        ctx.enter_context(tc.manual_schedule())
+
+        def kept(name, shape, dtype):
+            return keep.tile(shape, dtype, name=name, align_bytes=64)
+
+        ident = kept("ident", [P, P], F32)
+        warm = kept("warm", [P, 8], F32)
+        dbytes = [kept("dbytes%d" % j, [P, 2, D], U8) for j in range(2)] + [kept("dbytes2", [P, TPC, D], U8)]
+        dscale = kept("dscale", [P, PACK], F32)
+        wg_raw = kept("wg_raw", [P, H], U32)
+        wgs_raw = kept("wgs_raw", [P, H], U8)
+        wg_q = [kept("wg_q%d" % gr, [P, KP], U32) for gr in range(GROUPS)]
+        wg_s = [kept("wg_s%d" % gr, [P, KP], U8) for gr in range(GROUPS)]
+        bg_raw = kept("bg_raw", [P, GROUPS, PACK], BF16)
+        g_raw = kept("g_raw", [P, GROUPS, PACK], BF16)
+        neg_bg = kept("neg_bg", [P, GROUPS, PACK], F32)
+        gain = kept("gain", [P, GROUPS, PACK], F32)
+        h_sb = [kept("h%d" % c, [P, TPC, H], BF16) for c in range(CHUNKS)]
+        u_s = kept("u_s", [P, 3 * H], U8)
+        u_q = {(b, hf): kept("u%d_%d" % (b, hf), [P, GROUPS, KP], U32) for b in range(3) for hf in range(GROUPS)}
+        x_sb = [kept("x%d" % i, [P, 3 * H], BF16) for i in range(TILES)]
+        d_wide = [kept("d_wide%d" % i, [P, D], BF16) for i in range(TILES)]
+        d_grp = [kept("d_grp%d" % c, [P, CHUNK * PACK], BF16) for c in range(CHUNKS)]
+        d_q = [kept("d_q%d" % c, [P, CHUNK], U32) for c in range(CHUNKS)]
+        d_s = [kept("d_s%d" % c, [P, CHUNK], U8) for c in range(CHUNKS)]
+        hd_t = {(c, gr): kept("hd%d_%d" % (c, gr), [P, PACK, CHUNK], F32) for c in range(CHUNKS) for gr in range(GROUPS)}
+        planes = [kept("planes%d" % gr, [P, PACK, CHUNK], BF16) for gr in range(GROUPS)]
+        a_q = [kept("a_q%d" % j, [P, GROUPS * PAIR], U32) for j in range(TILES // 2)]
+        a_s = [kept("a_s%d" % j, [P, GROUPS * PAIR], U8) for j in range(TILES // 2)]
+
+        nc.vector.memset(warm[:], 0.0)
+        nc.vector.memset(wgs_raw[:].bitcast(I32), 0)
+        make_identity(nc, ident[:])
+        nc.vector.memset(u_s[:].bitcast(I32), 0)
+        nc.scalar.activation(out=warm[:, 0:1], in_=warm[:, 1:2], func=ACT.Exp)
+
+        def load_rows(tile, src, c):
+            nc.sync.dma_start(out=tile[:], in_=src[c * CHUNK:(c + 1) * CHUNK, :].rearrange("(i p) k -> p i k", p=P))
+
+        def load_u(b, hf):
+            lo = PACK * (b * H + hf * KP)
+            src = u_words.rearrange("g p n t -> p g (n t)")[:, :, lo:lo + PACK * KP]
+            nc.sync.dma_start(out=u_q[b, hf][:].bitcast(I32), in_=src.bitcast(I32))
+
+        def load_x(i):
+            nc.sync.dma_start(out=x_sb[i][:], in_=xp[i * P:(i + 1) * P, :])
+
+        for j in range(2):
+            nc.sync.dma_start(out=dbytes[j][:], in_=delta_bytes[j * PAIR:(j + 1) * PAIR, :].rearrange("(i p) k -> p i k", p=P))
+        nc.sync.dma_start(out=dscale[:], in_=delta_scale.rearrange("o (p t) -> p (o t)", t=PACK))
+        nc.sync.dma_start(out=wg_raw[:].bitcast(I32), in_=wg_words[0].rearrange("p n t -> p (n t)").bitcast(I32))
+        for q in range(4):
+            nc.sync.dma_start(out=wgs_raw[32 * q:32 * q + 4, :].bitcast(I32), in_=wg_scales[0, 4 * q:4 * q + 4, :].bitcast(I32))
+        nc.sync.dma_start(out=bg_raw[:], in_=bg.rearrange("(g p t) -> p g t", p=P, t=PACK))
+        load_rows(dbytes[2], delta_bytes, 1)
+        load_rows(h_sb[0], h, 0)
+        nc.sync.dma_start(out=g_raw[:], in_=g.rearrange("(g p t) -> p g t", p=P, t=PACK))
+        load_rows(h_sb[1], h, 1)
+        for q in range(4):
+            nc.sync.dma_start(out=u_s[32 * q:32 * q + 8, :].bitcast(I32), in_=u_scales[:, 4 * q:4 * q + 4, :].bitcast(I32))
+        for b in (R, Z, C):
+            load_u(b, 0)
+        load_x(0)
+        for b in (R, Z, C):
+            load_u(b, 1)
+        for i in range(1, TILES):
+            load_x(i)
+
+        def widen(i):
+            src = dbytes[i // 2][:, i % 2, :] if i < TPC else dbytes[2][:, i - TPC, :]
+            if i in (0, 2):
+                nc.vector.tensor_copy(out=d_wide[i][:], in_=src.bitcast(FP8))
+            else:
+                nc.scalar.copy(out=d_wide[i][:], in_=src.bitcast(FP8))
+
+        def turn_delta(j):
+            bank = psum.tile([P, 2, PAIR], F32, name="turn", tag="turn", bufs=4)
+            for k in range(2):
+                words = d_wide[2 * j + k][:].bitcast(F32)
+                for u in range(2):
+                    nc.tensor.transpose(bank[:, u, k * P:(k + 1) * P], words[:, u:D // 2:2], ident[:])
+            c, half = divmod(j, 2)
+            dst = d_grp[c][:, half * PAIR * PACK:(half + 1) * PAIR * PACK]
+            nc.vector.tensor_tensor(
+                out=dst.rearrange("p (k u e) -> p k u e", u=2, e=2),
+                in0=bank[:].rearrange("p u k -> p (u k)").bitcast(BF16).rearrange("p (u k e) -> p k u e", u=2, e=2),
+                in1=dscale[:].rearrange("p (u e) -> p u e", e=2).unsqueeze(1).to_broadcast([P, PAIR, 2, 2]),
+                op=ALU.mult,
+            )
+
+        def quant_delta(c):
+            nc.vector.quantize_mx(out=d_q[c][:].bitcast(FP8X4), scales=d_s[c][:], in_=d_grp[c][:])
+
+        def decay_exp(c, gr, t):
+            tag = "qa" if t % 2 == 0 else "qc"
+            bank = psum.tile([P, CHUNK], F32, name=tag, tag=tag)
+            cols = slice(t * P, (t + 1) * P)
+            nc.tensor.matmul_mx(
+                out=bank[:], lhsT=wg_q[gr][:, cols].bitcast(FP8X4), lhsT_scale=wg_s[gr][:, cols],
+                rhs=d_q[c][:].bitcast(FP8X4), rhs_scale=d_s[c][:], start=True, stop=True,
+            )
+            nc.scalar.activation(out=hd_t[c, gr][:, t, :], in_=bank[:], func=ACT.Exp, bias=neg_bg[:, gr, t:t + 1], scale=-1.0)
+
+        def turn_h(c, gr, u):
+            bank = psum.tile([P, CHUNK], F32, name="turn", tag="turn", bufs=4)
+            for k in range(TPC):
+                words = h_sb[c][:, k, :].bitcast(F32)
+                lo = gr * KP // 2
+                nc.tensor.transpose(bank[:, k * P:(k + 1) * P], words[:, lo + u:lo + KP // 2:2], ident[:])
+            return bank
+
+        def decay_h(c, gr, u, bank):
+            both = hd_t[c, gr][:, 2 * u:2 * u + 2, :]
+            nc.vector.scalar_tensor_tensor(
+                out=both, in0=both, scalar=1.0, in1=bank[:].bitcast(BF16).rearrange("p (k e) -> p e k", e=2),
+                op0=ALU.min, op1=ALU.mult,
+            )
+
+        a_grp = {}
+
+        def grp_tile(j):
+            if j not in a_grp:
+                tile = work.tile([P, GROUPS, PAIR * PACK], BF16, name="a_grp", tag="a_grp", bufs=1, align_bytes=64)
+                a_grp.setdefault(j, tile)
+            return a_grp[j]
+
+        def gain_direct(j, gr):
+            c, half = divmod(j, 2)
+            nc.gpsimd.tensor_tensor(
+                out=grp_tile(j)[:, gr, :].rearrange("p (k t) -> p k t", t=PACK),
+                in0=hd_t[c, gr][:, :, half * PAIR:(half + 1) * PAIR].rearrange("p t k -> p k t"),
+                in1=gain[:, gr, :].unsqueeze(1).to_broadcast([P, PAIR, PACK]),
+                op=ALU.mult,
+            )
+
+        def gain_plane(c, gr, t):
+            nc.scalar.activation(out=planes[gr][:, t, :], in_=hd_t[c, gr][:, t, :], func=ACT.Copy, scale=gain[:, gr, t:t + 1])
+
+        def weave(j, gr):
+            half = j % 2
+            nc.scalar.copy(
+                out=grp_tile(j)[:, gr, :].rearrange("p (k t) -> p k t", t=PACK),
+                in_=planes[gr][:, :, half * PAIR:(half + 1) * PAIR].rearrange("p t k -> p k t"),
+            )
+
+        def quant_act(j):
+            nc.vector.quantize_mx(out=a_q[j][:].bitcast(FP8X4), scales=a_s[j][:], in_=grp_tile(j)[:].rearrange("p g n -> p (g n)"))
+
+        def permute_wg(eng, gr):
+            eng.tensor_copy(
+                out=wg_q[gr][:].bitcast(I32).rearrange("p (t m) -> p t m", t=PACK),
+                in_=wg_raw[:, gr * KP:(gr + 1) * KP].bitcast(I32).rearrange("p (m t) -> p t m", t=PACK),
+            )
+            eng.tensor_copy(
+                out=wg_s[gr][:].rearrange("p (t m) -> p t m", t=PACK),
+                in_=wgs_raw[:, gr * KP:(gr + 1) * KP].rearrange("p (m t) -> p t m", t=PACK),
+            )
+
+        for i in range(TPC):
+            widen(i)
+        turn_delta(0)
+        turn_delta(1)
+        permute_wg(nc.vector, 0)
+        quant_delta(0)
+        nc.vector.tensor_scalar(out=neg_bg[:], in0=bg_raw[:], scalar1=-1.0, scalar2=None, op0=ALU.mult)
+        for i in range(TPC, TILES):
+            widen(i)
+        turn_delta(2)
+        permute_wg(nc.vector, 1)
+        for t in range(2):
+            decay_exp(0, 0, t)
+        turn_delta(3)
+        nc.vector.tensor_copy(out=gain[:], in_=g_raw[:])
+        quant_delta(1)
+
+        steps = [(c, gr, u) for c in range(CHUNKS) for gr in range(GROUPS) for u in range(2)]
+        for s, (c, gr, u) in enumerate(steps):
+            bank = turn_h(c, gr, u)
+            if s + 1 < len(steps):
+                nc_, ngr, nu = steps[s + 1]
+                for t in (2 * nu, 2 * nu + 1):
+                    decay_exp(nc_, ngr, t)
+            decay_h(c, gr, u, bank)
+            if c == 0 and u == 1:
+                gain_direct(0, gr)
+            if (c, gr, u) == (1, 1, 0):
+                quant_act(0)
+                gain_direct(1, 0)
+        nc.scalar.activation(out=warm[:, 2:3], in_=warm[:, 3:4], func=ACT.Sigmoid)
+
+        def product(n, b, tag):
+            i, hf = divmod(n, GROUPS)
+            j, k = divmod(i, 2)
+            bank = psum.tile([P, KP], F32, name=tag, tag=tag)
+            for gr in range(GROUPS):
+                toks = slice(gr * PAIR + k * P, gr * PAIR + (k + 1) * P)
+                lo = b * H + hf * KP
+                nc.tensor.matmul_mx(
+                    out=bank[:], lhsT=a_q[j][:, toks].bitcast(FP8X4), lhsT_scale=a_s[j][:, toks],
+                    rhs=u_q[b, hf][:, gr, :].bitcast(FP8X4), rhs_scale=u_s[4 * gr:P, lo:lo + KP],
+                    start=(gr == 0), stop=(gr == GROUPS - 1),
+                )
+            return bank
+
+        def x_part(n, b):
+            i, hf = divmod(n, GROUPS)
+            return x_sb[i][:, b * H + hf * KP:b * H + (hf + 1) * KP]
+
+        def turn_hd(n):
+            i, hf = divmod(n, GROUPS)
+            c, k = divmod(i, TPC)
+            bank = psum.tile([P, PACK, P], F32, name="turn", tag="turn", bufs=4)
+            for t in range(PACK):
+                nc.tensor.transpose(bank[:, t, :], hd_t[c, hf][:, t, k * P:(k + 1) * P], ident[:])
+            return bank[:].rearrange("p t m -> p m t")
+
+        def by_word(ap):
+            return ap.rearrange("p (m t) -> p m t", t=PACK)
+
+        hd_n, r_sb, z_sb, chain, banks = {}, {}, {}, {}, {}
+        whole = slice(0, KP)
+
+        def words_of(cols):
+            return slice(cols.start // PACK, cols.stop // PACK)
+
+        def products(n):
+            for b, tag in ((R, "qa"), (Z, "qa"), (C, "qc")):
+                banks.setdefault((n, b), product(n, b, tag))
+
+        def gate(n, b, store, tag, bufs):
+            tile = work.tile([P, KP], F32, name=tag, tag=tag, bufs=bufs)
+            store.setdefault(n, tile)
+            nc.vector.tensor_tensor(out=tile[:], in0=banks[n, b][:], in1=x_part(n, b), op=ALU.add)
+            nc.scalar.activation(out=tile[:], in_=tile[:], func=ACT.Sigmoid)
+
+        def reset(n):
+            tile = work.tile([P, KP], F32, name="ct", tag="ct")
+            chain.setdefault(n, tile)
+            nc.vector.tensor_tensor(out=tile[:], in0=banks[n, C][:], in1=r_sb[n][:], op=ALU.mult)
+
+        def add_xc(n, eng, cols):
+            eng.tensor_tensor(out=chain[n][:, cols], in0=chain[n][:, cols], in1=x_part(n, C)[:, cols], op=ALU.add)
+
+        def cand(n, cols):
+            nc.scalar.activation(out=chain[n][:, cols], in_=chain[n][:, cols], func=ACT.Tanh)
+
+        def diff(n, cols):
+            part = by_word(chain[n][:, cols])
+            nc.vector.tensor_tensor(out=part, in0=part, in1=hd_n[n][:, words_of(cols), :], op=ALU.subtract)
+
+        def mix(n, eng, cols):
+            eng.tensor_tensor(out=chain[n][:, cols], in0=chain[n][:, cols], in1=z_sb[n][:, cols], op=ALU.mult)
+
+        def finish(n, cols):
+            i, hf = divmod(n, GROUPS)
+            res = work.tile([P, KP], F32, name="res", tag="res")
+            nc.vector.tensor_tensor(
+                out=by_word(res[:, cols]), in0=by_word(chain[n][:, cols]), in1=hd_n[n][:, words_of(cols), :], op=ALU.add
+            )
+            nc.sync.dma_start(out=out[i * P:(i + 1) * P, hf * KP + cols.start:hf * KP + cols.stop], in_=res[:, cols])
+
+        last = UNITS - 1
+        for n in range(UNITS):
+            products(n)
+            if n >= 1:
+                hd_n.setdefault(n - 1, turn_hd(n - 1))
+            gate(n, R, r_sb, "r_sb", 2)
+            if n >= 1:
+                cand(n - 1, whole)
+            gate(n, Z, z_sb, "z_sb", 4)
+            if n < 4:
+                for t in (2 * (n % 2), 2 * (n % 2) + 1):
+                    gain_plane(1, n // 2, t)
+            if n in (4, 5):
+                weave(2, n - 4)
+            if n in (7, 8):
+                weave(3, n - 7)
+            if n >= 3:
+                finish(n - 3, whole)
+            if n in (2, 6, 10):
+                quant_act((n + 2) // 4)
+            reset(n)
+            if n < last:
+                add_xc(n, nc.gpsimd, whole)
+            if n == 0:
+                gain_direct(1, 1)
+            if n >= 1:
+                diff(n - 1, whole)
+                if n < last:
+                    mix(n - 1, nc.gpsimd, whole)
+
+        halves = (slice(0, KP // 2), slice(KP // 2, KP))
+        hd_n.setdefault(last, turn_hd(last))
+        for cols in halves:
+            add_xc(last, nc.vector, cols)
+            cand(last, cols)
+        mix(last - 1, nc.vector, whole)
+        finish(last - 2, whole)
+        for cols in halves:
+            diff(last, cols)
+        finish(last - 1, whole)
+        for cols in halves:
+            mix(last, nc.vector, cols)
+        for cols in halves:
+            finish(last, cols)

@@ -46,7 +46,7 @@ def tile_grudhiddendecayresetafterstep_w8_kernel(
         warm = kept("warm", [P, 8], F32)
         dbytes = [kept("dbytes%d" % j, [P, 2, D], U8) for j in range(2)] + [kept("dbytes2", [P, TPC, D], U8)]
         dscale = kept("dscale", [P, PACK], F32)
-        wg_raw = kept("wg_raw", [P, H], U32)
+        wg_raw = [kept("wg_raw%d" % gr, [P, KP], U32) for gr in range(GROUPS)]
         wgs_raw = kept("wgs_raw", [P, H], U8)
         wg_q = [kept("wg_q%d" % gr, [P, KP], U32) for gr in range(GROUPS)]
         wg_s = [kept("wg_s%d" % gr, [P, KP], U8) for gr in range(GROUPS)]
@@ -58,7 +58,8 @@ def tile_grudhiddendecayresetafterstep_w8_kernel(
         u_s = kept("u_s", [P, 3 * H], U8)
         u_q = {(b, hf): kept("u%d_%d" % (b, hf), [P, GROUPS, KP], U32) for b in range(3) for hf in range(GROUPS)}
         x_sb = [kept("x%d" % i, [P, 3 * H], BF16) for i in range(TILES)]
-        d_wide = [kept("d_wide%d" % i, [P, D], BF16) for i in range(TILES)]
+        d_val = [kept("d_val%d" % i, [P, D], BF16) for i in range(TILES)]
+        dscale_all = kept("dscale_all", [P, D], F32)
         d_grp = [kept("d_grp%d" % c, [P, CHUNK * PACK], BF16) for c in range(CHUNKS)]
         d_q = [kept("d_q%d" % c, [P, CHUNK], U32) for c in range(CHUNKS)]
         d_s = [kept("d_s%d" % c, [P, CHUNK], U8) for c in range(CHUNKS)]
@@ -84,14 +85,22 @@ def tile_grudhiddendecayresetafterstep_w8_kernel(
         def load_x(i):
             nc.sync.dma_start(out=x_sb[i][:], in_=xp[i * P:(i + 1) * P, :])
 
-        for j in range(2):
+        def load_wg(gr):
+            src = wg_words[0].rearrange("p n t -> p (n t)")[:, gr * KP * PACK:(gr + 1) * KP * PACK]
+            nc.sync.dma_start(out=wg_raw[gr][:].bitcast(I32), in_=src.bitcast(I32))
+
+        def load_pair(j):
             nc.sync.dma_start(out=dbytes[j][:], in_=delta_bytes[j * PAIR:(j + 1) * PAIR, :].rearrange("(i p) k -> p i k", p=P))
+
         nc.sync.dma_start(out=dscale[:], in_=delta_scale.rearrange("o (p t) -> p (o t)", t=PACK))
-        nc.sync.dma_start(out=wg_raw[:].bitcast(I32), in_=wg_words[0].rearrange("p n t -> p (n t)").bitcast(I32))
+        load_pair(0)
+        load_pair(1)
+        load_wg(0)
         for q in range(4):
             nc.sync.dma_start(out=wgs_raw[32 * q:32 * q + 4, :].bitcast(I32), in_=wg_scales[0, 4 * q:4 * q + 4, :].bitcast(I32))
         nc.sync.dma_start(out=bg_raw[:], in_=bg.rearrange("(g p t) -> p g t", p=P, t=PACK))
         load_rows(dbytes[2], delta_bytes, 1)
+        load_wg(1)
         load_rows(h_sb[0], h, 0)
         nc.sync.dma_start(out=g_raw[:], in_=g.rearrange("(g p t) -> p g t", p=P, t=PACK))
         load_rows(h_sb[1], h, 1)
@@ -105,27 +114,25 @@ def tile_grudhiddendecayresetafterstep_w8_kernel(
         for i in range(1, TILES):
             load_x(i)
 
-        def widen(i):
+        def spread_scale():
+            bank = psum.tile([P, PACK, P], F32, name="turn", tag="turn", bufs=4)
+            for t in range(PACK):
+                nc.tensor.transpose(bank[:, t, :], dscale[:, t:t + 1].to_broadcast([P, P]), ident[:])
+            nc.scalar.copy(out=dscale_all[:].rearrange("p (m t) -> p m t", t=PACK), in_=bank[:].rearrange("p t m -> p m t"))
+
+        def scale_delta(i):
             src = dbytes[i // 2][:, i % 2, :] if i < TPC else dbytes[2][:, i - TPC, :]
-            if i in (0, 2):
-                nc.vector.tensor_copy(out=d_wide[i][:], in_=src.bitcast(FP8))
-            else:
-                nc.scalar.copy(out=d_wide[i][:], in_=src.bitcast(FP8))
+            nc.vector.tensor_tensor(out=d_val[i][:], in0=src.bitcast(FP8), in1=dscale_all[:], op=ALU.mult)
 
         def turn_delta(j):
             bank = psum.tile([P, 2, PAIR], F32, name="turn", tag="turn", bufs=4)
             for k in range(2):
-                words = d_wide[2 * j + k][:].bitcast(F32)
+                words = d_val[2 * j + k][:].bitcast(F32)
                 for u in range(2):
                     nc.tensor.transpose(bank[:, u, k * P:(k + 1) * P], words[:, u:D // 2:2], ident[:])
             c, half = divmod(j, 2)
             dst = d_grp[c][:, half * PAIR * PACK:(half + 1) * PAIR * PACK]
-            nc.vector.tensor_tensor(
-                out=dst.rearrange("p (k u e) -> p k u e", u=2, e=2),
-                in0=bank[:].rearrange("p u k -> p (u k)").bitcast(BF16).rearrange("p (u k e) -> p k u e", u=2, e=2),
-                in1=dscale[:].rearrange("p (u e) -> p u e", e=2).unsqueeze(1).to_broadcast([P, PAIR, 2, 2]),
-                op=ALU.mult,
-            )
+            nc.scalar.copy(out=dst.bitcast(F32).rearrange("p (k u) -> p k u", u=2), in_=bank[:].rearrange("p u k -> p k u"))
 
         def quant_delta(c):
             nc.vector.quantize_mx(out=d_q[c][:].bitcast(FP8X4), scales=d_s[c][:], in_=d_grp[c][:])
@@ -188,43 +195,49 @@ def tile_grudhiddendecayresetafterstep_w8_kernel(
         def permute_wg(eng, gr):
             eng.tensor_copy(
                 out=wg_q[gr][:].bitcast(I32).rearrange("p (t m) -> p t m", t=PACK),
-                in_=wg_raw[:, gr * KP:(gr + 1) * KP].bitcast(I32).rearrange("p (m t) -> p t m", t=PACK),
+                in_=wg_raw[gr][:].bitcast(I32).rearrange("p (m t) -> p t m", t=PACK),
             )
             eng.tensor_copy(
                 out=wg_s[gr][:].rearrange("p (t m) -> p t m", t=PACK),
                 in_=wgs_raw[:, gr * KP:(gr + 1) * KP].rearrange("p (m t) -> p t m", t=PACK),
             )
 
-        for i in range(TPC):
-            widen(i)
-        turn_delta(0)
-        turn_delta(1)
+        spread_scale()
+        for j in range(2):
+            scale_delta(2 * j)
+            scale_delta(2 * j + 1)
+            turn_delta(j)
         permute_wg(nc.vector, 0)
-        quant_delta(0)
         nc.vector.tensor_scalar(out=neg_bg[:], in0=bg_raw[:], scalar1=-1.0, scalar2=None, op0=ALU.mult)
-        for i in range(TPC, TILES):
-            widen(i)
-        turn_delta(2)
-        permute_wg(nc.vector, 1)
-        for t in range(2):
+        scale_delta(4)
+        quant_delta(0)
+        for t in range(PACK):
             decay_exp(0, 0, t)
-        turn_delta(3)
+        permute_wg(nc.vector, 1)
+        for i in range(5, TILES):
+            scale_delta(i)
         nc.vector.tensor_copy(out=gain[:], in_=g_raw[:])
-        quant_delta(1)
 
-        steps = [(c, gr, u) for c in range(CHUNKS) for gr in range(GROUPS) for u in range(2)]
-        for s, (c, gr, u) in enumerate(steps):
-            bank = turn_h(c, gr, u)
-            if s + 1 < len(steps):
-                nc_, ngr, nu = steps[s + 1]
-                for t in (2 * nu, 2 * nu + 1):
-                    decay_exp(nc_, ngr, t)
-            decay_h(c, gr, u, bank)
-            if c == 0 and u == 1:
-                gain_direct(0, gr)
-            if (c, gr, u) == (1, 1, 0):
+        stages = [(c, gr) for c in range(CHUNKS) for gr in range(GROUPS)]
+        for s, (c, gr) in enumerate(stages):
+            pair = [turn_h(c, gr, u) for u in range(2)]
+            if s == 0:
+                turn_delta(2)
+                turn_delta(3)
+            if s == 1:
+                quant_delta(1)
+            if s + 1 < len(stages):
+                for t in range(PACK):
+                    decay_exp(stages[s + 1][0], stages[s + 1][1], t)
+            decay_h(c, gr, 0, pair[0])
+            if s < len(stages) - 1:
+                decay_h(c, gr, 1, pair[1])
+            if s == len(stages) - 2:
                 quant_act(0)
                 gain_direct(1, 0)
+                gain_direct(1, 1)
+            if c == 0:
+                gain_direct(0, gr)
         nc.scalar.activation(out=warm[:, 2:3], in_=warm[:, 3:4], func=ACT.Sigmoid)
 
         def product(n, b, tag):
@@ -273,7 +286,7 @@ def tile_grudhiddendecayresetafterstep_w8_kernel(
             nc.scalar.activation(out=tile[:], in_=tile[:], func=ACT.Sigmoid)
 
         def reset(n):
-            tile = work.tile([P, KP], F32, name="ct", tag="ct")
+            tile = work.tile([P, KP], F32, name="ct", tag="ct", bufs=5)
             chain.setdefault(n, tile)
             nc.vector.tensor_tensor(out=tile[:], in0=banks[n, C][:], in1=r_sb[n][:], op=ALU.mult)
 
@@ -299,46 +312,49 @@ def tile_grudhiddendecayresetafterstep_w8_kernel(
             nc.sync.dma_start(out=out[i * P:(i + 1) * P, hf * KP + cols.start:hf * KP + cols.stop], in_=res[:, cols])
 
         last = UNITS - 1
+        LD = 2
         for n in range(UNITS):
             products(n)
-            if n >= 1:
-                hd_n.setdefault(n - 1, turn_hd(n - 1))
+            if n >= LD:
+                hd_n.setdefault(n - LD, turn_hd(n - LD))
             gate(n, R, r_sb, "r_sb", 2)
-            if n >= 1:
-                cand(n - 1, whole)
-            gate(n, Z, z_sb, "z_sb", 4)
+            if n >= LD:
+                cand(n - LD, whole)
+            gate(n, Z, z_sb, "z_sb", 5)
             if n < 4:
-                for t in (2 * (n % 2), 2 * (n % 2) + 1):
-                    gain_plane(1, n // 2, t)
+                for k in (2 * n, 2 * n + 1):
+                    gain_plane(1, k // PACK, k % PACK)
             if n in (4, 5):
                 weave(2, n - 4)
-            if n in (7, 8):
-                weave(3, n - 7)
-            if n >= 3:
-                finish(n - 3, whole)
+            if n in (8, 9):
+                weave(3, n - 8)
+            if n == 0:
+                decay_h(c, gr, 1, pair[1])
+            if n >= LD + 2:
+                finish(n - LD - 2, whole)
+            reset(n)
             if n in (2, 6, 10):
                 quant_act((n + 2) // 4)
-            reset(n)
             if n < last:
                 add_xc(n, nc.gpsimd, whole)
-            if n == 0:
-                gain_direct(1, 1)
-            if n >= 1:
-                diff(n - 1, whole)
+            if n >= LD:
+                diff(n - LD, whole)
                 if n < last:
-                    mix(n - 1, nc.gpsimd, whole)
+                    mix(n - LD, nc.gpsimd, whole)
 
         halves = (slice(0, KP // 2), slice(KP // 2, KP))
+        cand(last - 1, whole)
+        add_xc(last, nc.vector, whole)
+        cand(last, whole)
+        mix(last - 2, nc.gpsimd, whole)
+        hd_n.setdefault(last - 1, turn_hd(last - 1))
+        finish(last - 3, whole)
         hd_n.setdefault(last, turn_hd(last))
-        for cols in halves:
-            add_xc(last, nc.vector, cols)
-            cand(last, cols)
+        diff(last - 1, whole)
+        diff(last, whole)
         mix(last - 1, nc.vector, whole)
         finish(last - 2, whole)
-        for cols in halves:
-            diff(last, cols)
+        mix(last, nc.vector, whole)
         finish(last - 1, whole)
-        for cols in halves:
-            mix(last, nc.vector, cols)
         for cols in halves:
             finish(last, cols)

@@ -44,7 +44,8 @@ def tile_grudhiddendecayresetafterstep_w8_kernel(
 
         ident = kept("ident", [P, P], F32)
         warm = kept("warm", [P, 8], F32)
-        dbytes = [kept("dbytes%d" % j, [P, 2, D], U8) for j in range(2)] + [kept("dbytes2", [P, TPC, D], U8)]
+        zeros = kept("zeros", [P, KP], BF16)
+        dbytes = [kept("dbytes%d" % j, [P, 2, D], U8) for j in range(TILES // 2)]
         dscale = kept("dscale", [P, PACK], F32)
         wg_raw = [kept("wg_raw%d" % gr, [P, KP], U32) for gr in range(GROUPS)]
         wgs_raw = kept("wgs_raw", [P, H], U8)
@@ -54,13 +55,16 @@ def tile_grudhiddendecayresetafterstep_w8_kernel(
         g_raw = kept("g_raw", [P, GROUPS, PACK], BF16)
         neg_bg = kept("neg_bg", [P, GROUPS, PACK], F32)
         gain = kept("gain", [P, GROUPS, PACK], F32)
-        h_sb = [kept("h%d" % c, [P, TPC, H], BF16) for c in range(CHUNKS)]
+        h_sb = {(c, gr): kept("h%d_%d" % (c, gr), [P, TPC, KP], BF16) for c in range(CHUNKS) for gr in range(GROUPS)}
         u_s = kept("u_s", [P, 3 * H], U8)
         u_q = {(b, hf): kept("u%d_%d" % (b, hf), [P, GROUPS, KP], U32) for b in range(3) for hf in range(GROUPS)}
         x_sb = [kept("x%d" % i, [P, 3 * H], BF16) for i in range(TILES)]
         d_val = [kept("d_val%d" % i, [P, D], BF16) for i in range(TILES)]
         dscale_all = kept("dscale_all", [P, D], F32)
-        d_grp = [kept("d_grp%d" % c, [P, CHUNK * PACK], BF16) for c in range(CHUNKS)]
+        d_grp = [
+            kept("d_grp0", [P, CHUNK * PACK], BF16),
+            work.tile([P, CHUNK * PACK], BF16, name="d_grp1", tag="a_grp", bufs=1, align_bytes=64),
+        ]
         d_q = [kept("d_q%d" % c, [P, CHUNK], U32) for c in range(CHUNKS)]
         d_s = [kept("d_s%d" % c, [P, CHUNK], U8) for c in range(CHUNKS)]
         hd_t = {(c, gr): kept("hd%d_%d" % (c, gr), [P, PACK, CHUNK], F32) for c in range(CHUNKS) for gr in range(GROUPS)}
@@ -68,8 +72,9 @@ def tile_grudhiddendecayresetafterstep_w8_kernel(
         a_q = [kept("a_q%d" % j, [P, GROUPS * PAIR], U32) for j in range(TILES // 2)]
         a_s = [kept("a_s%d" % j, [P, GROUPS * PAIR], U8) for j in range(TILES // 2)]
 
-        nc.vector.memset(warm[:], 0.0)
         nc.vector.memset(wgs_raw[:].bitcast(I32), 0)
+        nc.vector.memset(warm[:], 0.0)
+        nc.vector.memset(zeros[:], 0.0)
         make_identity(nc, ident[:])
         nc.vector.memset(u_s[:].bitcast(I32), 0)
         nc.scalar.activation(out=warm[:, 0:1], in_=warm[:, 1:2], func=ACT.Exp)
@@ -92,18 +97,25 @@ def tile_grudhiddendecayresetafterstep_w8_kernel(
         def load_pair(j):
             nc.sync.dma_start(out=dbytes[j][:], in_=delta_bytes[j * PAIR:(j + 1) * PAIR, :].rearrange("(i p) k -> p i k", p=P))
 
+        def load_h(c, gr):
+            src = h[c * CHUNK:(c + 1) * CHUNK, gr * KP:(gr + 1) * KP]
+            nc.sync.dma_start(out=h_sb[c, gr][:], in_=src.rearrange("(i p) k -> p i k", p=P))
+
         nc.sync.dma_start(out=dscale[:], in_=delta_scale.rearrange("o (p t) -> p (o t)", t=PACK))
-        load_pair(0)
-        load_pair(1)
         load_wg(0)
+        load_pair(0)
         for q in range(4):
             nc.sync.dma_start(out=wgs_raw[32 * q:32 * q + 4, :].bitcast(I32), in_=wg_scales[0, 4 * q:4 * q + 4, :].bitcast(I32))
+        load_pair(1)
+        load_h(0, 0)
+        load_pair(2)
         nc.sync.dma_start(out=bg_raw[:], in_=bg.rearrange("(g p t) -> p g t", p=P, t=PACK))
-        load_rows(dbytes[2], delta_bytes, 1)
+        load_pair(3)
         load_wg(1)
-        load_rows(h_sb[0], h, 0)
         nc.sync.dma_start(out=g_raw[:], in_=g.rearrange("(g p t) -> p g t", p=P, t=PACK))
-        load_rows(h_sb[1], h, 1)
+        load_h(0, 1)
+        load_h(1, 0)
+        load_h(1, 1)
         for q in range(4):
             nc.sync.dma_start(out=u_s[32 * q:32 * q + 8, :].bitcast(I32), in_=u_scales[:, 4 * q:4 * q + 4, :].bitcast(I32))
         for b in (R, Z, C):
@@ -114,6 +126,13 @@ def tile_grudhiddendecayresetafterstep_w8_kernel(
         for i in range(1, TILES):
             load_x(i)
 
+        def warm_pe(count):
+            if count == 0:
+                return
+            bank = psum.tile([P, KP], F32, name="qc", tag="qc")
+            for k in range(count):
+                nc.tensor.matmul(bank[:], lhsT=zeros[:, 0:P], rhs=zeros[:], start=True, stop=True)
+
         def spread_scale():
             bank = psum.tile([P, PACK, P], F32, name="turn", tag="turn", bufs=4)
             for t in range(PACK):
@@ -121,7 +140,7 @@ def tile_grudhiddendecayresetafterstep_w8_kernel(
             nc.scalar.copy(out=dscale_all[:].rearrange("p (m t) -> p m t", t=PACK), in_=bank[:].rearrange("p t m -> p m t"))
 
         def scale_delta(i):
-            src = dbytes[i // 2][:, i % 2, :] if i < TPC else dbytes[2][:, i - TPC, :]
+            src = dbytes[i // 2][:, i % 2, :]
             nc.vector.tensor_tensor(out=d_val[i][:], in0=src.bitcast(FP8), in1=dscale_all[:], op=ALU.mult)
 
         def turn_delta(j):
@@ -150,9 +169,8 @@ def tile_grudhiddendecayresetafterstep_w8_kernel(
         def turn_h(c, gr, u):
             bank = psum.tile([P, CHUNK], F32, name="turn", tag="turn", bufs=4)
             for k in range(TPC):
-                words = h_sb[c][:, k, :].bitcast(F32)
-                lo = gr * KP // 2
-                nc.tensor.transpose(bank[:, k * P:(k + 1) * P], words[:, lo + u:lo + KP // 2:2], ident[:])
+                words = h_sb[c, gr][:, k, :].bitcast(F32)
+                nc.tensor.transpose(bank[:, k * P:(k + 1) * P], words[:, u:KP // 2:2], ident[:])
             return bank
 
         def decay_h(c, gr, u, bank):
@@ -202,42 +220,53 @@ def tile_grudhiddendecayresetafterstep_w8_kernel(
                 in_=wgs_raw[:, gr * KP:(gr + 1) * KP].rearrange("p (m t) -> p t m", t=PACK),
             )
 
+        warm_pe(2)
         spread_scale()
+        warm_pe(4)
+        permute_wg(nc.vector, 0)
         for j in range(2):
             scale_delta(2 * j)
             scale_delta(2 * j + 1)
             turn_delta(j)
-        permute_wg(nc.vector, 0)
-        nc.vector.tensor_scalar(out=neg_bg[:], in0=bg_raw[:], scalar1=-1.0, scalar2=None, op0=ALU.mult)
+            warm_pe(2 if j == 0 else 0)
+        nc.scalar.activation(out=neg_bg[:], in_=bg_raw[:], func=ACT.Copy, scale=-1.0)
+        first = [turn_h(0, 0, 0)]
+        warm_pe(1)
         scale_delta(4)
+        scale_delta(5)
+        turn_delta(2)
+        warm_pe(0)
         quant_delta(0)
         for t in range(PACK):
             decay_exp(0, 0, t)
+        scale_delta(6)
+        scale_delta(7)
         permute_wg(nc.vector, 1)
-        for i in range(5, TILES):
-            scale_delta(i)
-        nc.vector.tensor_copy(out=gain[:], in_=g_raw[:])
+        nc.scalar.copy(out=gain[:], in_=g_raw[:])
 
+        first.extend([turn_h(0, 0, 1)])
+        turn_delta(3)
         stages = [(c, gr) for c in range(CHUNKS) for gr in range(GROUPS)]
+        pair = first
         for s, (c, gr) in enumerate(stages):
-            pair = [turn_h(c, gr, u) for u in range(2)]
-            if s == 0:
-                turn_delta(2)
-                turn_delta(3)
-            if s == 1:
-                quant_delta(1)
-            if s + 1 < len(stages):
+            more = s + 1 < len(stages)
+            if more:
                 for t in range(PACK):
                     decay_exp(stages[s + 1][0], stages[s + 1][1], t)
             decay_h(c, gr, 0, pair[0])
-            if s < len(stages) - 1:
+            if more:
                 decay_h(c, gr, 1, pair[1])
+            if s == 0:
+                quant_delta(1)
             if s == len(stages) - 2:
                 quant_act(0)
                 gain_direct(1, 0)
                 gain_direct(1, 1)
             if c == 0:
                 gain_direct(0, gr)
+            if more:
+                pair = [turn_h(stages[s + 1][0], stages[s + 1][1], u) for u in range(2)]
+        warm_pe(2)
         nc.scalar.activation(out=warm[:, 2:3], in_=warm[:, 3:4], func=ACT.Sigmoid)
 
         def product(n, b, tag):
@@ -275,8 +304,8 @@ def tile_grudhiddendecayresetafterstep_w8_kernel(
         def words_of(cols):
             return slice(cols.start // PACK, cols.stop // PACK)
 
-        def products(n):
-            for b, tag in ((R, "qa"), (Z, "qa"), (C, "qc")):
+        def products(n, which):
+            for b, tag in which:
                 banks.setdefault((n, b), product(n, b, tag))
 
         def gate(n, b, store, tag, bufs):
@@ -314,9 +343,10 @@ def tile_grudhiddendecayresetafterstep_w8_kernel(
         last = UNITS - 1
         LD = 2
         for n in range(UNITS):
-            products(n)
+            products(n, ((R, "qa"), (Z, "qa")))
             if n >= LD:
                 hd_n.setdefault(n - LD, turn_hd(n - LD))
+            products(n, ((C, "qc"),))
             gate(n, R, r_sb, "r_sb", 2)
             if n >= LD:
                 cand(n - LD, whole)

from contextlib import ExitStack

import concourse.mybir as mybir
from concourse.masks import make_identity

B, D, H = 1024, 512, 1024
FLOPS = 2 * B * D * H + 2 * B * H * 3 * H

F32 = mybir.dt.float32
BF16 = mybir.dt.bfloat16
I32 = mybir.dt.int32
U32 = mybir.dt.uint32
U8 = mybir.dt.uint8
FP8 = mybir.dt.float8_e4m3fn
FP8X4 = mybir.dt.float8_e4m3fn_x4
ACT = mybir.ActivationFunctionType
ALU = mybir.AluOpType

P = 128
PACK = 4
KP = P * PACK
TILES = B // P
CHUNK = 512
CHUNKS = B // CHUNK
TPC = CHUNK // P
GROUPS = H // KP
PAIR = 2 * P
UNITS = TILES * GROUPS
Z, R, C = 0, 1, 2


def tile_grudhiddendecayresetafterstep_w8_kernel(
    tc, xp, delta_bytes, delta_scale, h, wg_words, wg_scales, bg, g, u_words, u_scales, out
):
    nc = tc.nc
    with ExitStack() as ctx:
        keep = ctx.enter_context(tc.tile_pool(name="keep", bufs=1))
        work = ctx.enter_context(tc.tile_pool(name="work", bufs=4))
        psum = ctx.enter_context(tc.psum_pool(name="psum", bufs=2))
        ctx.enter_context(tc.manual_schedule())

        def kept(name, shape, dtype):
            return keep.tile(shape, dtype, name=name, align_bytes=64)

        ident = kept("ident", [P, P], F32)
        warm = kept("warm", [P, 8], F32)
        zeros = kept("zeros", [P, KP], BF16)
        dbytes = [kept("dbytes%d" % j, [P, 2, D], U8) for j in range(TILES // 2)]
        dscale = kept("dscale", [P, PACK], F32)
        wg_raw = [kept("wg_raw%d" % gr, [P, KP], U32) for gr in range(GROUPS)]
        wgs_raw = kept("wgs_raw", [P, H], U8)
        wg_q = [kept("wg_q%d" % gr, [P, KP], U32) for gr in range(GROUPS)]
        wg_s = [kept("wg_s%d" % gr, [P, KP], U8) for gr in range(GROUPS)]
        bg_raw = kept("bg_raw", [P, GROUPS, PACK], BF16)
        g_raw = kept("g_raw", [P, GROUPS, PACK], BF16)
        neg_bg = kept("neg_bg", [P, GROUPS, PACK], F32)
        gain = kept("gain", [P, GROUPS, PACK], F32)
        h_sb = {(c, gr): kept("h%d_%d" % (c, gr), [P, TPC, KP], BF16) for c in range(CHUNKS) for gr in range(GROUPS)}
        u_s = kept("u_s", [P, 3 * H], U8)
        u_q = {(b, hf): kept("u%d_%d" % (b, hf), [P, GROUPS, KP], U32) for b in range(3) for hf in range(GROUPS)}
        x_sb = [kept("x%d" % i, [P, 3 * H], BF16) for i in range(TILES)]
        d_val = [kept("d_val%d" % i, [P, D], BF16) for i in range(TILES)]
        dscale_all = kept("dscale_all", [P, D], F32)
        d_grp = [
            kept("d_grp0", [P, CHUNK * PACK], BF16),
            work.tile([P, CHUNK * PACK], BF16, name="d_grp1", tag="a_grp", bufs=1, align_bytes=64),
        ]
        d_q = [kept("d_q%d" % c, [P, CHUNK], U32) for c in range(CHUNKS)]
        d_s = [kept("d_s%d" % c, [P, CHUNK], U8) for c in range(CHUNKS)]
        hd_t = {(c, gr): kept("hd%d_%d" % (c, gr), [P, PACK, CHUNK], F32) for c in range(CHUNKS) for gr in range(GROUPS)}
        planes = [kept("planes%d" % gr, [P, PACK, CHUNK], BF16) for gr in range(GROUPS)]
        a_q = [kept("a_q%d" % j, [P, GROUPS * PAIR], U32) for j in range(TILES // 2)]
        a_s = [kept("a_s%d" % j, [P, GROUPS * PAIR], U8) for j in range(TILES // 2)]

        nc.vector.memset(wgs_raw[:].bitcast(I32), 0)
        nc.vector.memset(warm[:], 0.0)
        nc.vector.memset(zeros[:], 0.0)
        make_identity(nc, ident[:])
        nc.vector.memset(u_s[:].bitcast(I32), 0)
        nc.scalar.activation(out=warm[:, 0:1], in_=warm[:, 1:2], func=ACT.Exp)

        def load_rows(tile, src, c):
            nc.sync.dma_start(out=tile[:], in_=src[c * CHUNK:(c + 1) * CHUNK, :].rearrange("(i p) k -> p i k", p=P))

        def load_u(b, hf):
            lo = PACK * (b * H + hf * KP)
            src = u_words.rearrange("g p n t -> p g (n t)")[:, :, lo:lo + PACK * KP]
            nc.sync.dma_start(out=u_q[b, hf][:].bitcast(I32), in_=src.bitcast(I32))

        def load_x(i):
            nc.sync.dma_start(out=x_sb[i][:], in_=xp[i * P:(i + 1) * P, :])

        def load_wg(gr):
            src = wg_words[0].rearrange("p n t -> p (n t)")[:, gr * KP * PACK:(gr + 1) * KP * PACK]
            nc.sync.dma_start(out=wg_raw[gr][:].bitcast(I32), in_=src.bitcast(I32))

        def load_pair(j):
            nc.sync.dma_start(out=dbytes[j][:], in_=delta_bytes[j * PAIR:(j + 1) * PAIR, :].rearrange("(i p) k -> p i k", p=P))

        def load_h(c, gr):
            src = h[c * CHUNK:(c + 1) * CHUNK, gr * KP:(gr + 1) * KP]
            nc.sync.dma_start(out=h_sb[c, gr][:], in_=src.rearrange("(i p) k -> p i k", p=P))

        nc.sync.dma_start(out=dscale[:], in_=delta_scale.rearrange("o (p t) -> p (o t)", t=PACK))
        load_wg(0)
        load_pair(0)
        for q in range(4):
            nc.sync.dma_start(out=wgs_raw[32 * q:32 * q + 4, :].bitcast(I32), in_=wg_scales[0, 4 * q:4 * q + 4, :].bitcast(I32))
        load_pair(1)
        load_h(0, 0)
        load_pair(2)
        nc.sync.dma_start(out=bg_raw[:], in_=bg.rearrange("(g p t) -> p g t", p=P, t=PACK))
        load_pair(3)
        load_wg(1)
        nc.sync.dma_start(out=g_raw[:], in_=g.rearrange("(g p t) -> p g t", p=P, t=PACK))
        load_h(0, 1)
        load_h(1, 0)
        load_h(1, 1)
        for q in range(4):
            nc.sync.dma_start(out=u_s[32 * q:32 * q + 8, :].bitcast(I32), in_=u_scales[:, 4 * q:4 * q + 4, :].bitcast(I32))
        for b in (R, Z, C):
            load_u(b, 0)
        load_x(0)
        for b in (R, Z, C):
            load_u(b, 1)
        for i in range(1, TILES):
            load_x(i)

        def warm_pe(count):
            if count == 0:
                return
            bank = psum.tile([P, KP], F32, name="qc", tag="qc")
            for k in range(count):
                nc.tensor.matmul(bank[:], lhsT=zeros[:, 0:P], rhs=zeros[:], start=True, stop=True)

        def spread_scale():
            bank = psum.tile([P, PACK, P], F32, name="turn", tag="turn", bufs=4)
            for t in range(PACK):
                nc.tensor.transpose(bank[:, t, :], dscale[:, t:t + 1].to_broadcast([P, P]), ident[:])
            nc.scalar.copy(out=dscale_all[:].rearrange("p (m t) -> p m t", t=PACK), in_=bank[:].rearrange("p t m -> p m t"))

        def scale_delta(i):
            src = dbytes[i // 2][:, i % 2, :]
            nc.vector.tensor_tensor(out=d_val[i][:], in0=src.bitcast(FP8), in1=dscale_all[:], op=ALU.mult)

        def turn_delta(j):
            bank = psum.tile([P, 2, PAIR], F32, name="turn", tag="turn", bufs=4)
            for k in range(2):
                words = d_val[2 * j + k][:].bitcast(F32)
                for u in range(2):
                    nc.tensor.transpose(bank[:, u, k * P:(k + 1) * P], words[:, u:D // 2:2], ident[:])
            c, half = divmod(j, 2)
            dst = d_grp[c][:, half * PAIR * PACK:(half + 1) * PAIR * PACK]
            nc.scalar.copy(out=dst.bitcast(F32).rearrange("p (k u) -> p k u", u=2), in_=bank[:].rearrange("p u k -> p k u"))

        def quant_delta(c):
            nc.vector.quantize_mx(out=d_q[c][:].bitcast(FP8X4), scales=d_s[c][:], in_=d_grp[c][:])

        def decay_exp(c, gr, t):
            tag = "qa" if t % 2 == 0 else "qc"
            bank = psum.tile([P, CHUNK], F32, name=tag, tag=tag)
            cols = slice(t * P, (t + 1) * P)
            nc.tensor.matmul_mx(
                out=bank[:], lhsT=wg_q[gr][:, cols].bitcast(FP8X4), lhsT_scale=wg_s[gr][:, cols],
                rhs=d_q[c][:].bitcast(FP8X4), rhs_scale=d_s[c][:], start=True, stop=True,
            )
            nc.scalar.activation(out=hd_t[c, gr][:, t, :], in_=bank[:], func=ACT.Exp, bias=neg_bg[:, gr, t:t + 1], scale=-1.0)

        def turn_h(c, gr, u):
            bank = psum.tile([P, CHUNK], F32, name="turn", tag="turn", bufs=4)
            for k in range(TPC):
                words = h_sb[c, gr][:, k, :].bitcast(F32)
                nc.tensor.transpose(bank[:, k * P:(k + 1) * P], words[:, u:KP // 2:2], ident[:])
            return bank

        def decay_h(c, gr, u, bank):
            both = hd_t[c, gr][:, 2 * u:2 * u + 2, :]
            nc.vector.scalar_tensor_tensor(
                out=both, in0=both, scalar=1.0, in1=bank[:].bitcast(BF16).rearrange("p (k e) -> p e k", e=2),
                op0=ALU.min, op1=ALU.mult,
            )

        a_grp = {}

        def grp_tile(j):
            if j not in a_grp:
                tile = work.tile([P, GROUPS, PAIR * PACK], BF16, name="a_grp", tag="a_grp", bufs=1, align_bytes=64)
                a_grp.setdefault(j, tile)
            return a_grp[j]

        def gain_direct(j, gr):
            c, half = divmod(j, 2)
            nc.gpsimd.tensor_tensor(
                out=grp_tile(j)[:, gr, :].rearrange("p (k t) -> p k t", t=PACK),
                in0=hd_t[c, gr][:, :, half * PAIR:(half + 1) * PAIR].rearrange("p t k -> p k t"),
                in1=gain[:, gr, :].unsqueeze(1).to_broadcast([P, PAIR, PACK]),
                op=ALU.mult,
            )

        def gain_plane(c, gr, t):
            nc.scalar.activation(out=planes[gr][:, t, :], in_=hd_t[c, gr][:, t, :], func=ACT.Copy, scale=gain[:, gr, t:t + 1])

        def weave(j, gr):
            half = j % 2
            nc.scalar.copy(
                out=grp_tile(j)[:, gr, :].rearrange("p (k t) -> p k t", t=PACK),
                in_=planes[gr][:, :, half * PAIR:(half + 1) * PAIR].rearrange("p t k -> p k t"),
            )

        def quant_act(j):
            nc.vector.quantize_mx(out=a_q[j][:].bitcast(FP8X4), scales=a_s[j][:], in_=grp_tile(j)[:].rearrange("p g n -> p (g n)"))

        def permute_wg(eng, gr):
            eng.tensor_copy(
                out=wg_q[gr][:].bitcast(I32).rearrange("p (t m) -> p t m", t=PACK),
                in_=wg_raw[gr][:].bitcast(I32).rearrange("p (m t) -> p t m", t=PACK),
            )
            eng.tensor_copy(
                out=wg_s[gr][:].rearrange("p (t m) -> p t m", t=PACK),
                in_=wgs_raw[:, gr * KP:(gr + 1) * KP].rearrange("p (m t) -> p t m", t=PACK),
            )

        warm_pe(2)
        spread_scale()
        warm_pe(4)
        permute_wg(nc.vector, 0)
        for j in range(2):
            scale_delta(2 * j)
            scale_delta(2 * j + 1)
            turn_delta(j)
            warm_pe(2 if j == 0 else 0)
        nc.scalar.activation(out=neg_bg[:], in_=bg_raw[:], func=ACT.Copy, scale=-1.0)
        first = [turn_h(0, 0, 0)]
        warm_pe(1)
        scale_delta(4)
        scale_delta(5)
        turn_delta(2)
        warm_pe(0)
        quant_delta(0)
        for t in range(PACK):
            decay_exp(0, 0, t)
        scale_delta(6)
        scale_delta(7)
        permute_wg(nc.vector, 1)
        nc.scalar.copy(out=gain[:], in_=g_raw[:])

        first.extend([turn_h(0, 0, 1)])
        turn_delta(3)
        stages = [(c, gr) for c in range(CHUNKS) for gr in range(GROUPS)]
        pair = first
        for s, (c, gr) in enumerate(stages):
            more = s + 1 < len(stages)
            if more:
                for t in range(PACK):
                    decay_exp(stages[s + 1][0], stages[s + 1][1], t)
            decay_h(c, gr, 0, pair[0])
            if more:
                decay_h(c, gr, 1, pair[1])
            if s == 0:
                quant_delta(1)
            if s == len(stages) - 2:
                quant_act(0)
                gain_direct(1, 0)
                gain_direct(1, 1)
            if c == 0:
                gain_direct(0, gr)
            if more:
                pair = [turn_h(stages[s + 1][0], stages[s + 1][1], u) for u in range(2)]
        warm_pe(2)
        nc.scalar.activation(out=warm[:, 2:3], in_=warm[:, 3:4], func=ACT.Sigmoid)

        def product(n, b, tag):
            i, hf = divmod(n, GROUPS)
            j, k = divmod(i, 2)
            bank = psum.tile([P, KP], F32, name=tag, tag=tag)
            for gr in range(GROUPS):
                toks = slice(gr * PAIR + k * P, gr * PAIR + (k + 1) * P)
                lo = b * H + hf * KP
                nc.tensor.matmul_mx(
                    out=bank[:], lhsT=a_q[j][:, toks].bitcast(FP8X4), lhsT_scale=a_s[j][:, toks],
                    rhs=u_q[b, hf][:, gr, :].bitcast(FP8X4), rhs_scale=u_s[4 * gr:P, lo:lo + KP],
                    start=(gr == 0), stop=(gr == GROUPS - 1),
                )
            return bank

        def x_part(n, b):
            i, hf = divmod(n, GROUPS)
            return x_sb[i][:, b * H + hf * KP:b * H + (hf + 1) * KP]

        def turn_hd(n):
            i, hf = divmod(n, GROUPS)
            c, k = divmod(i, TPC)
            bank = psum.tile([P, PACK, P], F32, name="turn", tag="turn", bufs=4)
            for t in range(PACK):
                nc.tensor.transpose(bank[:, t, :], hd_t[c, hf][:, t, k * P:(k + 1) * P], ident[:])
            return bank[:].rearrange("p t m -> p m t")

        def by_word(ap):
            return ap.rearrange("p (m t) -> p m t", t=PACK)

        hd_n, r_sb, z_sb, chain, banks = {}, {}, {}, {}, {}
        whole = slice(0, KP)

        def words_of(cols):
            return slice(cols.start // PACK, cols.stop // PACK)

        def products(n, which):
            for b, tag in which:
                banks.setdefault((n, b), product(n, b, tag))

        def gate(n, b, store, tag, bufs):
            tile = work.tile([P, KP], F32, name=tag, tag=tag, bufs=bufs)
            store.setdefault(n, tile)
            nc.vector.tensor_tensor(out=tile[:], in0=banks[n, b][:], in1=x_part(n, b), op=ALU.add)
            nc.scalar.activation(out=tile[:], in_=tile[:], func=ACT.Sigmoid)

        def reset(n):
            tile = work.tile([P, KP], F32, name="ct", tag="ct", bufs=5)
            chain.setdefault(n, tile)
            nc.vector.tensor_tensor(out=tile[:], in0=banks[n, C][:], in1=r_sb[n][:], op=ALU.mult)

        def add_xc(n, eng, cols):
            eng.tensor_tensor(out=chain[n][:, cols], in0=chain[n][:, cols], in1=x_part(n, C)[:, cols], op=ALU.add)

        def cand(n, cols):
            nc.scalar.activation(out=chain[n][:, cols], in_=chain[n][:, cols], func=ACT.Tanh)

        def diff(n, cols):
            part = by_word(chain[n][:, cols])
            nc.vector.tensor_tensor(out=part, in0=part, in1=hd_n[n][:, words_of(cols), :], op=ALU.subtract)

        def mix(n, eng, cols):
            eng.tensor_tensor(out=chain[n][:, cols], in0=chain[n][:, cols], in1=z_sb[n][:, cols], op=ALU.mult)

        def finish(n, cols):
            i, hf = divmod(n, GROUPS)
            res = work.tile([P, KP], F32, name="res", tag="res")
            nc.vector.tensor_tensor(
                out=by_word(res[:, cols]), in0=by_word(chain[n][:, cols]), in1=hd_n[n][:, words_of(cols), :], op=ALU.add
            )
            nc.sync.dma_start(out=out[i * P:(i + 1) * P, hf * KP + cols.start:hf * KP + cols.stop], in_=res[:, cols])

        last = UNITS - 1
        LD = 2
        for n in range(UNITS):
            products(n, ((R, "qa"), (Z, "qa")))
            if n >= LD:
                hd_n.setdefault(n - LD, turn_hd(n - LD))
            products(n, ((C, "qc"),))
            gate(n, R, r_sb, "r_sb", 2)
            if n >= LD:
                cand(n - LD, whole)
            gate(n, Z, z_sb, "z_sb", 5)
            if n < 4:
                for k in (2 * n, 2 * n + 1):
                    gain_plane(1, k // PACK, k % PACK)
            if n in (4, 5):
                weave(2, n - 4)
            if n in (8, 9):
                weave(3, n - 8)
            if n == 0:
                decay_h(c, gr, 1, pair[1])
            if n >= LD + 2:
                finish(n - LD - 2, whole)
            reset(n)
            if n in (2, 6, 10):
                quant_act((n + 2) // 4)
            if n < last:
                add_xc(n, nc.gpsimd, whole)
            if n >= LD:
                diff(n - LD, whole)
                if n < last:
                    mix(n - LD, nc.gpsimd, whole)

        halves = (slice(0, KP // 2), slice(KP // 2, KP))
        cand(last - 1, whole)
        add_xc(last, nc.vector, whole)
        cand(last, whole)
        mix(last - 2, nc.gpsimd, whole)
        hd_n.setdefault(last - 1, turn_hd(last - 1))
        finish(last - 3, whole)
        hd_n.setdefault(last, turn_hd(last))
        diff(last - 1, whole)
        diff(last, whole)
        mix(last - 1, nc.vector, whole)
        finish(last - 2, whole)
        mix(last, nc.vector, whole)
        finish(last - 1, whole)
        for cols in halves:
            finish(last, cols)
